import numpy as np, ml_dtypes
CORES = [5,21,45,77,85,101,109,125,133,141,189,213]
N = 12
import mx_ref
NC = 256
WID = [130,208,168,236,162,128,226,184,216,150,240,256]
BF = ml_dtypes.bfloat16
def setup_inputs(rng):
    def f(*shape):
        return mx_ref.flush((rng.standard_normal(shape, dtype=np.float32) * np.exp2(rng.integers(-2, 3, shape[:-1] + (1,)))).astype(BF))
    return {"w": f(N, 128, 512), "x": f(N, 128, 4 * NC)}
def setup_inputs_blocks(rng):
    d = setup_inputs(rng)
    for k in ("w", "x"): d[k] = mx_ref.spread(d[k], rng, 4)
    return d
def setup_inputs_wide(rng):
    d = setup_inputs(rng)
    for k in ("w", "x"): d[k] = mx_ref.flush((d[k].astype(np.float32) * np.exp2(rng.integers(-8, 9, (N, 1, 1))).astype(np.float32)).astype(BF))
    return d
def setup_inputs_zeros(rng):
    d = setup_inputs(rng); v = d["x"].reshape(N, 128, -1, 4).copy()
    v[np.broadcast_to((rng.random((N, 1, v.shape[2], 1)) < 0.33), v.shape)] = 0
    d["x"] = v.reshape(d["x"].shape)
    return d
def reference(w, x):
    OFF = [sum(WID[:j]) for j in range(N + 1)]
    y = np.zeros((N, 128, OFF[N]), np.float32)
    for r in range(N):
        qw = mx_ref.quantize(w[r])
        for j in range(N):
            y[r][:, OFF[j]:OFF[j + 1]] = mx_ref.matmul(qw, mx_ref.quantize(x[j][:, :4 * WID[j]]))
    return {"y": y}

from concourse.bass import DstId, RemoteDMATransfer
from concourse.mybir import dt, ActivationFunctionType

N = 12
SLOT = 256
YCOLS = 2304
BANKS = 8
BANK = 512
SIM_CORES = 256
DIRECT = 3

SCRATCH = {
    "xb": ("sbuf", [128, 4 * SLOT], "bfloat16"),
    "wb": ("sbuf", [128, 512], "bfloat16"),
    "wq": ("sbuf", [128, 128], "float8_e4m3fn_x4"),
    "ws": ("sbuf", [128, 128], "uint8"),
    "gq": ("sbuf", [128, N * SLOT], "float8_e4m3fn_x4"),
    "gs": ("sbuf", [128, N * SLOT], "uint8"),
    "ys": ("sbuf", [128, YCOLS], "float32"),
    "ps": ("psum", [128, BANKS * BANK], "float32"),
}
SEMAPHORES = (["ldx", "ldw", "qx", "qw", "hs", "hc", "sent", "sty", "stz"]
              + ["arr%d" % j for j in range(N)] + ["mm%d" % i for i in range(N)] + ["cp%d" % i for i in range(N)])

_CACHE = {}


def _count(mask):
    return bin(mask).count("1")


def _common_mask(topo, src, dsts):
    m = topo.mask(src, dsts[0])
    for d in dsts[1:]:
        m &= topo.mask(src, d)
    return m


def _plan(T, topo):
    if "plan" in _CACHE:
        return _CACHE["plan"]
    cores = [int(c) for c in T.cores]
    wid = T.tables["WID"]
    n = len(cores)
    plane_a = [r for r in range(n) if r == 0 or topo.same_plane(cores[0], cores[r])]
    plane_b = [r for r in range(n) if r not in plane_a]
    direct = {}
    helpers = {}
    when = {}
    for own, other in ((plane_a, plane_b), (plane_b, plane_a)):
        m, pairs = len(own), len(other) // 2
        for i, j in enumerate(own):
            me = cores[j]
            chip = [c for c in range(SIM_CORES)
                    if c != me and topo.host(c) == topo.host(me) and topo.chip(c) == topo.chip(me)]
            port = [c for c in chip if all(topo.may_write(c, cores[d]) for d in other)]
            near = [c for c in port if topo.die(c) == topo.die(me)][0]
            far = [c for c in port if topo.die(c) != topo.die(me)][0]
            plain = [c for c in chip if topo.die(c) != topo.die(me) and c not in port][0]
            p, b = divmod(i, 2)
            turn = [(p - s) % pairs for s in range(pairs)]
            direct[j] = [own[(i + k) % m] for k in range(1, DIRECT + 1)]
            helpers[j] = [(far, [other[2 * q + 1 - b] for q in turn]),
                          (near, [other[2 * q + b] for q in turn]),
                          (plain, [own[(i + k) % m] for k in range(DIRECT + 1, m)])]
            for s, d in enumerate(direct[j]):
                when[(j, d)] = (0, s, 0, 0)
            for h, (c, dsts) in enumerate(helpers[j]):
                for s, d in enumerate(dsts):
                    last = s == pairs - 1
                    when[(j, d)] = (1, s, wid[j] if last else 0, 0 if h < 2 else 1)
    order, stores = {}, {}
    for d in range(n):
        seq = [d] + sorted([j for j in range(n) if j != d], key=lambda j: when[(j, d)] + (j,))
        order[d] = seq
        grp, i = [], 0
        while i < n:
            j = seq[i]
            if (i + 1 < n and j != d and when[(j, d)][0] == 1 and when[(j, d)][2:] == (0, 0)
                    and when[(seq[i + 1], d)] == when[(j, d)] and seq[i + 1] == j + 1):
                grp.append([i, i + 1])
                i += 2
            else:
                grp.append([i])
                i += 1
        stores[d] = grp
    relay = {}
    for j in range(n):
        for c, dsts in helpers[j]:
            relay[c] = (j, dsts)
    _CACHE["plan"] = {"cores": cores, "direct": direct, "helpers": helpers, "relay": relay, "order": order, "stores": stores}
    return _CACHE["plan"]


def _send(g, T, topo, src, dsts, view, mask, sem):
    ids = []
    for d in dsts:
        rid, pid = topo.addr(d, src)
        ids.append(DstId(rid=rid, pnc=pid))
    g.remote_dma_fused([RemoteDMATransfer(dst_ids=ids, dma_engine_mask=mask, remote_sem=sem, srcs=[view()],
                                          dsts=[view() for _ in dsts])], local_sem=T.sem.sent)


def rank_program(g, core, T, topo):
    plan = _plan(T, topo)
    cores, wid = plan["cores"], T.tables["WID"]

    def plane_of(j):
        return lambda: T.gs[:, j * SLOT:j * SLOT + wid[j]]

    def codes_of(j):
        return lambda: T.gq[:, j * SLOT:j * SLOT + wid[j]].bitcast(dt.uint8)

    def masks_of(j):
        away = _common_mask(topo, cores[j], [cores[d] for d in plan["direct"][j]])
        home = _common_mask(topo, cores[j], [c for c, _ in plan["helpers"][j]]) & ~away
        return away, home

    if core in plan["relay"]:
        j, ranks = plan["relay"][core]
        dsts = [cores[d] for d in ranks]
        mask = _common_mask(topo, core, dsts)
        fed = _count(masks_of(j)[1])
        g.wait_ge(T.sem.hs, fed)
        _send(g, T, topo, core, dsts, plane_of(j), mask, T.sem["arr%d" % j])
        g.wait_ge(T.sem.hc, fed)
        _send(g, T, topo, core, dsts, codes_of(j), mask, T.sem["arr%d" % j])
        g.wait_ge(T.sem.sent, 2 * _count(mask))
        return

    r = T.rank_of(core)
    if r is None:
        return
    w = wid[r]
    off = [sum(wid[:j]) for j in range(N + 1)]

    g.sync.dma_start(T.xb[:, :4 * w], T.x[:, :4 * w]).then_inc(T.sem.ldx, 16)
    g.sync.dma_start(T.wb[:], T.w[:]).then_inc(T.sem.ldw, 16)
    g.vector.wait_ge(T.sem.ldx, 16)
    g.vector.quantize_mx(T.gq[:, r * SLOT:r * SLOT + w], T.gs[:, r * SLOT:r * SLOT + w], T.xb[:, :4 * w]).then_inc(T.sem.qx, 1)
    g.vector.wait_ge(T.sem.ldw, 16)
    g.vector.quantize_mx(T.wq[:], T.ws[:], T.wb[:]).then_inc(T.sem.qw, 1)

    away = [cores[d] for d in plan["direct"][r]]
    home = [c for c, _ in plan["helpers"][r]]
    m_away, m_home = masks_of(r)
    g.wait_ge(T.sem.qx, 1)
    _send(g, T, topo, core, home, plane_of(r), m_home, T.sem.hs)
    _send(g, T, topo, core, home, codes_of(r), m_home, T.sem.hc)
    _send(g, T, topo, core, away, plane_of(r), m_away, T.sem["arr%d" % r])
    _send(g, T, topo, core, away, codes_of(r), m_away, T.sem["arr%d" % r])

    sender = {}
    for j in range(N):
        for d in plan["direct"][j]:
            sender[(j, d)] = cores[j]
        for c, ranks in plan["helpers"][j]:
            for d in ranks:
                sender[(j, d)] = c
    order = plan["order"][r]
    last_of = {grp[-1]: grp for grp in plan["stores"][r]}
    stored = {"sty": 0, "stz": 0}
    g.tensor.wait_ge(T.sem.qw, 1)
    for i, j in enumerate(order):
        n, s, b = wid[j], j * SLOT, (i % BANKS) * BANK
        if j == r:
            g.tensor.wait_ge(T.sem.qx, 1)
        else:
            g.tensor.wait_ge(T.sem["arr%d" % j], 2 * _count(topo.mask(sender[(j, r)], core)))
        if i >= BANKS:
            g.tensor.wait_ge(T.sem["cp%d" % (i - BANKS)], 1)
        g.tensor.matmul_mx(T.ps[:, b:b + n], T.wq[:], T.ws[:], T.gq[:, s:s + n], T.gs[:, s:s + n], True, True).then_inc(
            T.sem["mm%d" % i], 1)
        if i % 2 == 0:
            g.vector.wait_ge(T.sem["mm%d" % i], 1)
            g.vector.tensor_copy(T.ys[:, off[j]:off[j + 1]], T.ps[:, b:b + n]).then_inc(T.sem["cp%d" % i], 1)
        else:
            g.scalar.wait_ge(T.sem["mm%d" % i], 1)
            g.scalar.activation(T.ys[:, off[j]:off[j + 1]], T.ps[:, b:b + n], ActivationFunctionType.Copy).then_inc(
                T.sem["cp%d" % i], 1)
        if i in last_of:
            grp = last_of[i]
            lo, hi = min(off[order[k]] for k in grp), max(off[order[k] + 1] for k in grp)
            q, sem = (g.scalar, "stz") if (len(grp) == 1 and i % 2 == 1) else (g.sync, "sty")
            for k in grp:
                q.wait_ge(T.sem["cp%d" % k], 1)
            q.dma_start(T.y[:, lo:hi], T.ys[:, lo:hi]).then_inc(T.sem[sem], 16)
            stored[sem] += 16
    g.sync.wait_ge(T.sem.sty, stored["sty"])
    g.scalar.wait_ge(T.sem.stz, stored["stz"])
    g.wait_ge(T.sem.sent, 2 * (_count(m_home) + _count(m_away)))
